import numpy as np, ml_dtypes
CORES = [17,57,65,89,97,121]
N = 6
import mx_ref
NC = 512
BF = ml_dtypes.bfloat16
def setup_inputs(rng):
    def f(*shape):
        return mx_ref.flush((rng.standard_normal(shape, dtype=np.float32) * np.exp2(rng.integers(-2, 3, shape[:-1] + (1,)))).astype(BF))
    return {"w": f(N, 128, N * 512), "x": f(N, 128, 4 * NC)}
def setup_inputs_blocks(rng):
    d = setup_inputs(rng)
    for k in ("w", "x"): d[k] = mx_ref.spread(d[k], rng, 2)
    return d
def setup_inputs_wide(rng):
    d = setup_inputs(rng)
    for k in ("w", "x"): d[k] = mx_ref.flush((d[k].astype(np.float32) * np.exp2(rng.integers(-8, 9, (N, 1, 1))).astype(np.float32)).astype(BF))
    return d
def setup_inputs_zeros(rng):
    d = setup_inputs(rng); v = d["x"].reshape(N, 128, -1, 4).copy()
    v[np.broadcast_to((rng.random((N, 1, v.shape[2], 1)) < 0.33), v.shape)] = 0
    d["x"] = v.reshape(d["x"].shape)
    return d
def reference(w, x):
    QX = [mx_ref.quantize(x[j]) for j in range(N)]
    y = np.zeros((N, 128, NC), np.float32)
    for r in range(N):
        for j in range(N):
            p = mx_ref.matmul(mx_ref.quantize(w[r][:, 512 * j:512 * j + 512]), QX[j])
            y[r] = p if j == 0 else y[r] + p
    return {"y": y}

@@ -1,0 +1,236 @@
+from concourse.bass import DstId, RemoteDMATransfer
+from concourse.mybir import dt, ActivationFunctionType
+
+N = 6
+NC = 512
+WT = 128
+SIM_CORES = 128
+
+QX = [(0, 256), (256, 512)]
+MM = [(0, 256), (256, 512)]
+PIECES = [("s", 0, 256), ("c", 0, 256), ("s", 256, 512), ("c", 256, 512)]
+
+S_CALLS = [
+    [(0, ("role", [("p1", 0)]), (0, 2)), (2, ("role", [("p0", 0), ("f0", 0)]), (1, 2))],
+    [(1, ("role", [("p1", 0)]), (0, 2)), (3, ("role", [("p0", 0), ("f0", 0)]), (1, 2))],
+    [(0, ("same", [0, 1]), (0, 1))],
+    [(1, ("same", [0, 1]), (0, 1))],
+]
+HELP = {
+    ("p1", 0): [[(0, ("relay", [1, 2]), (0, 1))], [(1, ("relay", [1, 2]), (0, 1))],
+                [(0, ("cross", [0]), (0, 1))], [(1, ("cross", [0]), (0, 1))]],
+    ("p0", 0): [[(2, ("relay", [1, 2]), (0, 1))], [(3, ("relay", [1, 2]), (0, 1))],
+                [(2, ("cross", [0]), (0, 1))], [(3, ("cross", [0]), (0, 1))]],
+    ("f0", 0): [[(2, ("same", [0, 1]), (0, 1))], [(3, ("same", [0, 1]), (0, 1))]],
+}
+W_LOADS = [(0, 6)]
+
+SCRATCH = {
+    "xb": ("sbuf", [128, 4 * NC], "bfloat16"),
+    "wb": ("sbuf", [128, 4 * WT * N], "bfloat16"),
+    "xq": ("sbuf", [128, NC * N], "float8_e4m3fn_x4"),
+    "xs": ("sbuf", [128, NC * N], "uint8"),
+    "wq": ("sbuf", [128, WT * N], "float8_e4m3fn_x4"),
+    "ws": ("sbuf", [128, WT * N], "uint8"),
+    "ps": ("psum", [128, 512 * len(MM)], "float32"),
+    "yb": ("sbuf", [128, NC], "float32"),
+}
+SEMAPHORES = (["ldx%d" % k for k in range(len(QX))] + ["qx%d" % k for k in range(len(QX))]
+              + ["ldw%d" % k for k in range(len(W_LOADS))] + ["qw%d" % j for j in range(N)]
+              + ["arr%d_%d" % (j, p) for j in range(N) for p in range(len(PIECES))]
+              + ["mm%d" % k for k in range(len(MM))] + ["cp%d" % k for k in range(len(MM))]
+              + ["st%d" % k for k in range(len(MM))] + ["sent"])
+
+
+def _bits(mask):
+    return [b for b in range(mask.bit_length()) if (mask >> b) & 1]
+
+
+def _part(mask, i, n):
+    b = _bits(mask)
+    m = len(b) // n
+    out = 0
+    for e in b[i * m:(i + 1) * m]:
+        out |= 1 << e
+    return out
+
+
+def _count(mask):
+    return len(_bits(mask))
+
+
+def _places(cores, topo, j):
+    s = cores[j]
+    same = [d for d in cores if topo.same_plane(topo.chip(d), topo.chip(s))]
+    cross = [d for d in cores if d != s and d not in same]
+    mine = sorted(same + [s], key=cores.index)
+    i = mine.index(s)
+    same_rot = [mine[(i + 1 + t) % len(mine)] for t in range(len(mine) - 1)]
+    cross_rot = [cross[(i + t) % len(cross)] for t in range(len(cross))]
+    kinds = {"p1": [], "p0": [], "f1": [], "f0": []}
+    for c in range(SIM_CORES):
+        if topo.chip(c) != topo.chip(s) or c == s:
+            continue
+        port = all(topo.may_write(c, d) for d in cross)
+        kinds[("p" if port else "f") + ("1" if topo.die(c) == topo.die(s) else "0")].append(c)
+    return kinds, same_rot, cross_rot
+
+
+def _relay(topo, src, d, t):
+    cand = [c for c in range(SIM_CORES) if topo.mates(topo.chip(c), topo.chip(d))
+            and topo.die(c) == topo.die(src) and topo.may_write(c, d)]
+    return cand[t % len(cand)]
+
+
+def build_plan(cores, topo):
+    raw, expect, eta = {}, {}, {}
+    for j in range(N):
+        s = cores[j]
+        kinds, same_rot, cross_rot = _places(cores, topo, j)
+
+        def emit(src, table, stage):
+            for ci, call in enumerate(table):
+                trs, waits = [], []
+                for (p, (what, idx), (i, n)) in call:
+                    if what == "role":
+                        dsts = [kinds[k][m] for (k, m) in idx]
+                    elif what == "relay":
+                        dsts = [_relay(topo, src, cross_rot[t], t) for t in idx]
+                    else:
+                        dsts = [(same_rot if what == "same" else cross_rot)[t] for t in idx]
+                    allowed = topo.mask(src, dsts[0])
+                    for d in dsts:
+                        allowed &= topo.mask(src, d)
+                    mask = _part(allowed, i, n)
+                    trs.append((j, p, dsts, mask))
+                    if (j, p) not in waits:
+                        waits.append((j, p))
+                    for pos, d in enumerate(dsts):
+                        expect[(d, j, p)] = expect.get((d, j, p), 0) + _count(mask)
+                        eta[(d, j, p)] = max(eta.get((d, j, p), 0), stage * 100 + ci * 10 + pos)
+                        if what == "relay":
+                            f = cross_rot[idx[pos]]
+                            fm = topo.mask(d, f)
+                            raw.setdefault(d, []).append(((stage + 1, ci, pos), [(j, p)], [(j, p, [f], fm)]))
+                            expect[(f, j, p)] = expect.get((f, j, p), 0) + _count(fm)
+                            eta[(f, j, p)] = max(eta.get((f, j, p), 0), (stage + 1) * 100 + ci * 10 + pos)
+                raw.setdefault(src, []).append(((stage, ci, 0), waits, trs))
+
+        emit(s, S_CALLS, 0)
+        for (k, m), table in HELP.items():
+            emit(kinds[k][m], table, 1)
+    calls = {c: [(w, t) for (_pr, w, t) in sorted(v, key=lambda e: e[0])] for c, v in raw.items()}
+    return calls, expect, eta
+
+
+def _view(T, j, p):
+    kind, a, b = PIECES[p]
+    if kind == "c":
+        return T.xq[:, NC * j + a:NC * j + b].bitcast(dt.uint8)
+    return T.xs[:, NC * j + a:NC * j + b]
+
+
+def _overlap(a, b, c, d):
+    return a < d and c < b
+
+
+def rank_program(g, core, T, topo):
+    cores = list(T.cores)
+    calls, expect, eta = build_plan(cores, topo)
+    rank = T.rank_of(core)
+    mine = calls.get(core, [])
+    if rank is None and not mine:
+        return
+
+    if rank is not None:
+        for k, (a, b) in enumerate(QX):
+            g.sync.dma_start(T.xb[:, 4 * a:4 * b], T.x[:, 4 * a:4 * b]).then_inc(T.sem["ldx%d" % k], 16)
+        for k, (a, b) in enumerate(W_LOADS):
+            g.sync.dma_start(T.wb[:, 4 * WT * a:4 * WT * b], T.w[:, 4 * WT * a:4 * WT * b]).then_inc(T.sem["ldw%d" % k], 16)
+        for k, (a, b) in enumerate(QX):
+            g.vector.wait_ge(T.sem["ldx%d" % k], 16)
+            g.vector.quantize_mx(T.xq[:, NC * rank + a:NC * rank + b], T.xs[:, NC * rank + a:NC * rank + b],
+                                 T.xb[:, 4 * a:4 * b]).then_inc(T.sem["qx%d" % k], 1)
+
+    sent = 0
+    waited = set()
+    for waits, trs in mine:
+        for (j, p) in waits:
+            if cores[j] == core:
+                for k, (a, b) in enumerate(QX):
+                    if _overlap(a, b, PIECES[p][1], PIECES[p][2]) and ("q", k) not in waited:
+                        waited.add(("q", k))
+                        g.wait_ge(T.sem["qx%d" % k], 1)
+            elif (j, p) not in waited:
+                waited.add((j, p))
+                g.wait_ge(T.sem["arr%d_%d" % (j, p)], expect[(core, j, p)])
+        if len(trs) == 1 and len(trs[0][2]) == 1:
+            j, p, dsts, mask = trs[0]
+            rid, pid, _se = topo.addr(dsts[0])
+            g.remote_dma(_view(T, j, p), _view(T, j, p), T.sem["arr%d_%d" % (j, p)], T.sem.sent, pid, rid, mask)
+            sent += _count(mask)
+        else:
+            lst = []
+            for (j, p, dsts, mask) in trs:
+                ids = [DstId(rid=topo.addr(d)[0], pnc=topo.addr(d)[1]) for d in dsts]
+                lst.append(RemoteDMATransfer(dst_ids=ids, dma_engine_mask=mask, remote_sem=T.sem["arr%d_%d" % (j, p)],
+                                             srcs=[_view(T, j, p)], dsts=[_view(T, j, p) for _d in dsts]))
+                sent += _count(mask)
+            g.remote_dma_fused(lst, local_sem=T.sem.sent)
+    if sent:
+        g.wait_ge(T.sem.sent, sent)
+    if rank is None:
+        return
+
+    seen = set()
+    for j in [rank] + [j for j in range(N) if j != rank]:
+        for k, (a, b) in enumerate(W_LOADS):
+            if a <= j < b and k not in seen:
+                seen.add(k)
+                g.vector.wait_ge(T.sem["ldw%d" % k], 16)
+        g.vector.quantize_mx(T.wq[:, WT * j:WT * j + WT], T.ws[:, WT * j:WT * j + WT],
+                             T.wb[:, 4 * WT * j:4 * WT * j + 4 * WT]).then_inc(T.sem["qw%d" % j], 1)
+
+    items = []
+    for j in range(N):
+        for k, (a, b) in enumerate(MM):
+            ps = [p for p in range(len(PIECES)) if _overlap(a, b, PIECES[p][1], PIECES[p][2])]
+            e = -1 if j == rank else max(eta[(core, j, p)] for p in ps)
+            items.append((e, j, k, ps))
+    items.sort()
+    done = [0] * len(MM)
+    tw = set()
+    for (e, j, k, ps) in items:
+        a, b = MM[k]
+        if ("w", j) not in tw:
+            tw.add(("w", j))
+            g.tensor.wait_ge(T.sem["qw%d" % j], 1)
+        if j == rank:
+            for q, (c, d) in enumerate(QX):
+                if _overlap(a, b, c, d) and ("q", q) not in tw:
+                    tw.add(("q", q))
+                    g.tensor.wait_ge(T.sem["qx%d" % q], 1)
+        else:
+            for p in ps:
+                if (j, p) not in tw:
+                    tw.add((j, p))
+                    g.tensor.wait_ge(T.sem["arr%d_%d" % (j, p)], expect[(core, j, p)])
+        ins = g.tensor.matmul_mx(T.ps[:, 512 * k:512 * k + (b - a)], T.wq[:, WT * j:WT * j + WT], T.ws[:, WT * j:WT * j + WT],
+                                 T.xq[:, NC * j + a:NC * j + b], T.xs[:, NC * j + a:NC * j + b], done[k] == 0, done[k] == N - 1)
+        done[k] += 1
+        if done[k] == N:
+            ins.then_inc(T.sem["mm%d" % k], 1)
+
+    for k, (a, b) in enumerate(MM):
+        if k % 2 == 0:
+            g.vector.wait_ge(T.sem["mm%d" % k], 1)
+            g.vector.tensor_copy(T.yb[:, a:b], T.ps[:, 512 * k:512 * k + (b - a)]).then_inc(T.sem["cp%d" % k], 1)
+            q = g.sync
+        else:
+            g.scalar.wait_ge(T.sem["mm%d" % k], 1)
+            g.scalar.activation(T.yb[:, a:b], T.ps[:, 512 * k:512 * k + (b - a)], ActivationFunctionType.Copy).then_inc(T.sem["cp%d" % k], 1)
+            q = g.scalar
+        q.wait_ge(T.sem["cp%d" % k], 1)
+        q.dma_start(T.y[:, a:b], T.yb[:, a:b]).then_inc(T.sem["st%d" % k], 16)
+    for k in range(len(MM)):
+        (g.sync if k % 2 == 0 else g.scalar).wait_ge(T.sem["st%d" % k], 16)

@@ -6,15 +6,16 @@ NC = 512
 WT = 128
 SIM_CORES = 128
 
-QX = [(0, 256), (256, 512)]
+QX = [(256, 512), (0, 256)]
 MM = [(0, 256), (256, 512)]
 PIECES = [("s", 0, 256), ("c", 0, 256), ("s", 256, 512), ("c", 256, 512)]
 
 S_CALLS = [
-    [(0, ("role", [("p1", 0)]), (0, 2)), (2, ("role", [("p0", 0), ("f0", 0)]), (1, 2))],
-    [(1, ("role", [("p1", 0)]), (0, 2)), (3, ("role", [("p0", 0), ("f0", 0)]), (1, 2))],
+    [(2, ("role", [("p0", 0), ("f0", 0)]), (1, 2))],
+    [(0, ("role", [("p1", 0)]), (0, 2))],
+    [(1, ("role", [("p1", 0)]), (0, 2)), (3, ("role", [("p0", 0)]), (1, 2))],
     [(0, ("same", [0, 1]), (0, 1))],
-    [(1, ("same", [0, 1]), (0, 1))],
+    [(1, ("same", [0, 1]), (0, 1)), (3, ("role", [("f0", 0)]), (1, 2))],
 ]
 HELP = {
     ("p1", 0): [[(0, ("relay", [1, 2]), (0, 1))], [(1, ("relay", [1, 2]), (0, 1))],
@@ -144,7 +145,8 @@ def rank_program(g, core, T, topo):
 
     if rank is not None:
         for k, (a, b) in enumerate(QX):
-            g.sync.dma_start(T.xb[:, 4 * a:4 * b], T.x[:, 4 * a:4 * b]).then_inc(T.sem["ldx%d" % k], 16)
+            q = g.sync if k % 2 == 0 else g.scalar
+            q.dma_start(T.xb[:, 4 * a:4 * b], T.x[:, 4 * a:4 * b]).then_inc(T.sem["ldx%d" % k], 16)
         for k, (a, b) in enumerate(W_LOADS):
             g.sync.dma_start(T.wb[:, 4 * WT * a:4 * WT * b], T.w[:, 4 * WT * a:4 * WT * b]).then_inc(T.sem["ldw%d" % k], 16)
         for k, (a, b) in enumerate(QX):

from concourse.bass import DstId, RemoteDMATransfer
from concourse.mybir import dt, ActivationFunctionType

N = 6
NC = 512
WT = 128
SIM_CORES = 128

QX = [(256, 512), (0, 256)]
MM = [(0, 256), (256, 512)]
PIECES = [("s", 0, 256), ("c", 0, 256), ("s", 256, 512), ("c", 256, 512)]

S_CALLS = [
    [(2, ("role", [("p0", 0), ("f0", 0)]), (1, 2))],
    [(0, ("role", [("p1", 0)]), (0, 2))],
    [(1, ("role", [("p1", 0)]), (0, 2)), (3, ("role", [("p0", 0)]), (1, 2))],
    [(0, ("same", [0, 1]), (0, 1))],
    [(1, ("same", [0, 1]), (0, 1)), (3, ("role", [("f0", 0)]), (1, 2))],
]
HELP = {
    ("p1", 0): [[(0, ("relay", [1, 2]), (0, 1))], [(1, ("relay", [1, 2]), (0, 1))],
                [(0, ("cross", [0]), (0, 1))], [(1, ("cross", [0]), (0, 1))]],
    ("p0", 0): [[(2, ("relay", [1, 2]), (0, 1))], [(3, ("relay", [1, 2]), (0, 1))],
                [(2, ("cross", [0]), (0, 1))], [(3, ("cross", [0]), (0, 1))]],
    ("f0", 0): [[(2, ("same", [0, 1]), (0, 1))], [(3, ("same", [0, 1]), (0, 1))]],
}
W_LOADS = [(0, 6)]

SCRATCH = {
    "xb": ("sbuf", [128, 4 * NC], "bfloat16"),
    "wb": ("sbuf", [128, 4 * WT * N], "bfloat16"),
    "xq": ("sbuf", [128, NC * N], "float8_e4m3fn_x4"),
    "xs": ("sbuf", [128, NC * N], "uint8"),
    "wq": ("sbuf", [128, WT * N], "float8_e4m3fn_x4"),
    "ws": ("sbuf", [128, WT * N], "uint8"),
    "ps": ("psum", [128, 512 * len(MM)], "float32"),
    "yb": ("sbuf", [128, NC], "float32"),
}
SEMAPHORES = (["ldx%d" % k for k in range(len(QX))] + ["qx%d" % k for k in range(len(QX))]
              + ["ldw%d" % k for k in range(len(W_LOADS))] + ["qw%d" % j for j in range(N)]
              + ["arr%d_%d" % (j, p) for j in range(N) for p in range(len(PIECES))]
              + ["mm%d" % k for k in range(len(MM))] + ["cp%d" % k for k in range(len(MM))]
              + ["st%d" % k for k in range(len(MM))] + ["sent"])


def _bits(mask):
    return [b for b in range(mask.bit_length()) if (mask >> b) & 1]


def _part(mask, i, n):
    b = _bits(mask)
    m = len(b) // n
    out = 0
    for e in b[i * m:(i + 1) * m]:
        out |= 1 << e
    return out


def _count(mask):
    return len(_bits(mask))


def _places(cores, topo, j):
    s = cores[j]
    same = [d for d in cores if topo.same_plane(topo.chip(d), topo.chip(s))]
    cross = [d for d in cores if d != s and d not in same]
    mine = sorted(same + [s], key=cores.index)
    i = mine.index(s)
    same_rot = [mine[(i + 1 + t) % len(mine)] for t in range(len(mine) - 1)]
    cross_rot = [cross[(i + t) % len(cross)] for t in range(len(cross))]
    kinds = {"p1": [], "p0": [], "f1": [], "f0": []}
    for c in range(SIM_CORES):
        if topo.chip(c) != topo.chip(s) or c == s:
            continue
        port = all(topo.may_write(c, d) for d in cross)
        kinds[("p" if port else "f") + ("1" if topo.die(c) == topo.die(s) else "0")].append(c)
    return kinds, same_rot, cross_rot


def _relay(topo, src, d, t):
    cand = [c for c in range(SIM_CORES) if topo.mates(topo.chip(c), topo.chip(d))
            and topo.die(c) == topo.die(src) and topo.may_write(c, d)]
    return cand[t % len(cand)]


def build_plan(cores, topo):
    raw, expect, eta = {}, {}, {}
    for j in range(N):
        s = cores[j]
        kinds, same_rot, cross_rot = _places(cores, topo, j)

        def emit(src, table, stage):
            for ci, call in enumerate(table):
                trs, waits = [], []
                for (p, (what, idx), (i, n)) in call:
                    if what == "role":
                        dsts = [kinds[k][m] for (k, m) in idx]
                    elif what == "relay":
                        dsts = [_relay(topo, src, cross_rot[t], t) for t in idx]
                    else:
                        dsts = [(same_rot if what == "same" else cross_rot)[t] for t in idx]
                    allowed = topo.mask(src, dsts[0])
                    for d in dsts:
                        allowed &= topo.mask(src, d)
                    mask = _part(allowed, i, n)
                    trs.append((j, p, dsts, mask))
                    if (j, p) not in waits:
                        waits.append((j, p))
                    for pos, d in enumerate(dsts):
                        expect[(d, j, p)] = expect.get((d, j, p), 0) + _count(mask)
                        eta[(d, j, p)] = max(eta.get((d, j, p), 0), stage * 100 + ci * 10 + pos)
                        if what == "relay":
                            f = cross_rot[idx[pos]]
                            fm = topo.mask(d, f)
                            raw.setdefault(d, []).append(((stage + 1, ci, pos), [(j, p)], [(j, p, [f], fm)]))
                            expect[(f, j, p)] = expect.get((f, j, p), 0) + _count(fm)
                            eta[(f, j, p)] = max(eta.get((f, j, p), 0), (stage + 1) * 100 + ci * 10 + pos)
                raw.setdefault(src, []).append(((stage, ci, 0), waits, trs))

        emit(s, S_CALLS, 0)
        for (k, m), table in HELP.items():
            emit(kinds[k][m], table, 1)
    calls = {c: [(w, t) for (_pr, w, t) in sorted(v, key=lambda e: e[0])] for c, v in raw.items()}
    return calls, expect, eta


def _view(T, j, p):
    kind, a, b = PIECES[p]
    if kind == "c":
        return T.xq[:, NC * j + a:NC * j + b].bitcast(dt.uint8)
    return T.xs[:, NC * j + a:NC * j + b]


def _overlap(a, b, c, d):
    return a < d and c < b


def rank_program(g, core, T, topo):
    cores = list(T.cores)
    calls, expect, eta = build_plan(cores, topo)
    rank = T.rank_of(core)
    mine = calls.get(core, [])
    if rank is None and not mine:
        return

    if rank is not None:
        for k, (a, b) in enumerate(QX):
            q = g.sync if k % 2 == 0 else g.scalar
            q.dma_start(T.xb[:, 4 * a:4 * b], T.x[:, 4 * a:4 * b]).then_inc(T.sem["ldx%d" % k], 16)
        for k, (a, b) in enumerate(W_LOADS):
            g.sync.dma_start(T.wb[:, 4 * WT * a:4 * WT * b], T.w[:, 4 * WT * a:4 * WT * b]).then_inc(T.sem["ldw%d" % k], 16)
        for k, (a, b) in enumerate(QX):
            g.vector.wait_ge(T.sem["ldx%d" % k], 16)
            g.vector.quantize_mx(T.xq[:, NC * rank + a:NC * rank + b], T.xs[:, NC * rank + a:NC * rank + b],
                                 T.xb[:, 4 * a:4 * b]).then_inc(T.sem["qx%d" % k], 1)

    sent = 0
    waited = set()
    for waits, trs in mine:
        for (j, p) in waits:
            if cores[j] == core:
                for k, (a, b) in enumerate(QX):
                    if _overlap(a, b, PIECES[p][1], PIECES[p][2]) and ("q", k) not in waited:
                        waited.add(("q", k))
                        g.wait_ge(T.sem["qx%d" % k], 1)
            elif (j, p) not in waited:
                waited.add((j, p))
                g.wait_ge(T.sem["arr%d_%d" % (j, p)], expect[(core, j, p)])
        if len(trs) == 1 and len(trs[0][2]) == 1:
            j, p, dsts, mask = trs[0]
            rid, pid, _se = topo.addr(dsts[0])
            g.remote_dma(_view(T, j, p), _view(T, j, p), T.sem["arr%d_%d" % (j, p)], T.sem.sent, pid, rid, mask)
            sent += _count(mask)
        else:
            lst = []
            for (j, p, dsts, mask) in trs:
                ids = [DstId(rid=topo.addr(d)[0], pnc=topo.addr(d)[1]) for d in dsts]
                lst.append(RemoteDMATransfer(dst_ids=ids, dma_engine_mask=mask, remote_sem=T.sem["arr%d_%d" % (j, p)],
                                             srcs=[_view(T, j, p)], dsts=[_view(T, j, p) for _d in dsts]))
                sent += _count(mask)
            g.remote_dma_fused(lst, local_sem=T.sem.sent)
    if sent:
        g.wait_ge(T.sem.sent, sent)
    if rank is None:
        return

    seen = set()
    for j in [rank] + [j for j in range(N) if j != rank]:
        for k, (a, b) in enumerate(W_LOADS):
            if a <= j < b and k not in seen:
                seen.add(k)
                g.vector.wait_ge(T.sem["ldw%d" % k], 16)
        g.vector.quantize_mx(T.wq[:, WT * j:WT * j + WT], T.ws[:, WT * j:WT * j + WT],
                             T.wb[:, 4 * WT * j:4 * WT * j + 4 * WT]).then_inc(T.sem["qw%d" % j], 1)

    items = []
    for j in range(N):
        for k, (a, b) in enumerate(MM):
            ps = [p for p in range(len(PIECES)) if _overlap(a, b, PIECES[p][1], PIECES[p][2])]
            e = -1 if j == rank else max(eta[(core, j, p)] for p in ps)
            items.append((e, j, k, ps))
    items.sort()
    done = [0] * len(MM)
    tw = set()
    for (e, j, k, ps) in items:
        a, b = MM[k]
        if ("w", j) not in tw:
            tw.add(("w", j))
            g.tensor.wait_ge(T.sem["qw%d" % j], 1)
        if j == rank:
            for q, (c, d) in enumerate(QX):
                if _overlap(a, b, c, d) and ("q", q) not in tw:
                    tw.add(("q", q))
                    g.tensor.wait_ge(T.sem["qx%d" % q], 1)
        else:
            for p in ps:
                if (j, p) not in tw:
                    tw.add((j, p))
                    g.tensor.wait_ge(T.sem["arr%d_%d" % (j, p)], expect[(core, j, p)])
        ins = g.tensor.matmul_mx(T.ps[:, 512 * k:512 * k + (b - a)], T.wq[:, WT * j:WT * j + WT], T.ws[:, WT * j:WT * j + WT],
                                 T.xq[:, NC * j + a:NC * j + b], T.xs[:, NC * j + a:NC * j + b], done[k] == 0, done[k] == N - 1)
        done[k] += 1
        if done[k] == N:
            ins.then_inc(T.sem["mm%d" % k], 1)

    for k, (a, b) in enumerate(MM):
        if k % 2 == 0:
            g.vector.wait_ge(T.sem["mm%d" % k], 1)
            g.vector.tensor_copy(T.yb[:, a:b], T.ps[:, 512 * k:512 * k + (b - a)]).then_inc(T.sem["cp%d" % k], 1)
            q = g.sync
        else:
            g.scalar.wait_ge(T.sem["mm%d" % k], 1)
            g.scalar.activation(T.yb[:, a:b], T.ps[:, 512 * k:512 * k + (b - a)], ActivationFunctionType.Copy).then_inc(T.sem["cp%d" % k], 1)
            q = g.scalar
        q.wait_ge(T.sem["cp%d" % k], 1)
        q.dma_start(T.y[:, a:b], T.yb[:, a:b]).then_inc(T.sem["st%d" % k], 16)
    for k in range(len(MM)):
        (g.sync if k % 2 == 0 else g.scalar).wait_ge(T.sem["st%d" % k], 16)
